import numpy as np
import ml_dtypes


def mxq(x, axis, fmt="e4m3"):
    dtype, down = {"e4m3": (ml_dtypes.float8_e4m3fn, 7), "e5m2": (ml_dtypes.float8_e5m2, 14)}[fmt]
    v = np.moveaxis(np.asarray(x, np.float32).astype(ml_dtypes.bfloat16).astype(np.float64), axis, -1)
    blocks = v.reshape(v.shape[:-1] + (-1, 32))
    amax = np.abs(blocks).max(-1, keepdims=True)
    byte = np.maximum(np.where(amax > 0, np.frexp(amax)[1] - 1 + 127, 0) - down, 1)
    scale = np.exp2(byte - 127.0)
    codes = (blocks / scale).astype(np.float32).astype(dtype).astype(np.float64)
    return np.moveaxis((codes * scale).reshape(v.shape), -1, axis)


WIDE = False


def mx_kscale(k):
    if not WIDE:
        return np.ones(k)
    levels = np.array([10, -10, 5, -5, 0])
    if k % 512:
        return np.exp2(np.random.permutation(np.resize(levels, k // 32))).repeat(32)
    a = np.empty((k // 512, 16))
    for p in range(k // 512):
        a[p, :8] = np.random.permutation(np.resize(levels, 8))
        for g in range(8):
            far = levels[np.abs(levels - a[p, g]) >= 10]
            a[p, g + 8] = far[np.random.randint(len(far))]
    return np.exp2(a.ravel()).repeat(32)


BF16 = ml_dtypes.bfloat16


def bf(x):
    return np.asarray(x, np.float32).astype(BF16)


def f64(x):
    return np.asarray(x).astype(np.float64)


E2M1 = np.array([0.0, 0.5, 1.0, 1.5, 2.0, 3.0, 4.0, 6.0, -0.0, -0.5, -1.0, -1.5, -2.0, -3.0, -4.0, -6.0])


def pack_weight(w, fmt):
    k, n = w.shape
    w = f64(bf(w)).reshape(k // 32, 32, n)
    amax = np.abs(w).max(1)
    if fmt == "e4m3":
        byte = np.frexp(amax)[1] - 1 + 127 - 7
    else:
        mant, ex = np.frexp(amax / 6.0)
        byte = np.where(mant > 0.5, ex, ex - 1) + 127
    byte = np.clip(np.where(amax > 0, byte, 1), 1, 254)
    scaled = (w * np.exp2(127.0 - byte)[:, None, :]).reshape(k, n).astype(np.float32)
    by_word = np.ascontiguousarray(scaled.reshape(k // 512, 128, 4, n).transpose(0, 1, 3, 2))
    if fmt == "e4m3":
        words = by_word.astype(ml_dtypes.float8_e4m3fn).view(np.uint8)
    else:
        c = by_word.astype(ml_dtypes.float4_e2m1fn).view(np.uint8) & 0xF
        words = c[..., 0::2] | (c[..., 1::2] << 4)
    return np.ascontiguousarray(words), np.ascontiguousarray(byte.astype(np.uint8).reshape(k // 512, 16, n))


def unpack_weight(words, scales, fmt):
    g, p, n, _ = words.shape
    if fmt == "e4m3":
        vals = np.ascontiguousarray(words).view(ml_dtypes.float8_e4m3fn).astype(np.float64)
    else:
        nib = np.empty((g, p, n, 4), np.uint8)
        nib[..., 0::2] = words & 0xF
        nib[..., 1::2] = words >> 4
        vals = E2M1[nib]
    vals = vals * np.repeat(np.exp2(scales.astype(np.float64) - 127.0), 8, axis=1)[..., None]
    return vals.transpose(0, 1, 3, 2).reshape(g * 512, n)

E4M3FN = np.array([(-1.0 if i & 128 else 1.0) * ((1.0 + (i & 7) / 8.0) * 2.0 ** (((i >> 3) & 15) - 7) if i & 120 else (i & 7) * 2.0 ** -9) for i in range(256)])


def e4m3fn_bytes(y):
    return np.clip(np.asarray(y, np.float64), -448.0, 448.0).astype(np.float32).astype(ml_dtypes.float8_e4m3fn).view(np.uint8)


def e4m3fn_values(b):
    return E4M3FN[b]


P, K, W, N = 1024, 512, 1024, 512


def sigmoid(a):
    return 1.0 / (1.0 + np.exp(-a))


def draw0():
    sv, sr, sl = mx_kscale(K), mx_kscale(K), mx_kscale(K)
    t = mx_kscale(W)
    c = 1.0 / np.sqrt(K)
    v = bf(np.random.standard_normal((P, K)) * sv)
    psi_words, psi_scales = pack_weight(np.random.standard_normal((K, W)) * c / sv[:, None], "e4m3")
    r = bf(np.random.standard_normal((P, K)) * 2.0 * sr)
    phi_words, phi_scales = pack_weight(np.random.standard_normal((K, W)) * c / sr[:, None] * t, "e4m3")
    q = bf(np.random.uniform(0.5, 1.5, W))
    l = bf(np.random.standard_normal((N, K)) * sl)
    theta_words, theta_scales = pack_weight(np.random.standard_normal((K, W)) * c / sl[:, None] / t, "e4m3")
    return {
        "v": v,
        "psi_words": psi_words,
        "psi_scales": psi_scales,
        "r": r,
        "phi_words": phi_words,
        "phi_scales": phi_scales,
        "q": q,
        "l": l,
        "theta_words": theta_words,
        "theta_scales": theta_scales,
    }


def core(v, psi_words, psi_scales, r, phi_words, phi_scales, q, l, theta_words, theta_scales):
    num_dirs = psi_words.shape[2]
    vis = sigmoid(mxq(f64(v), 1, "e4m3") @ unpack_weight(psi_words, psi_scales, "e4m3"))
    refl = mxq(f64(r), 1, "e4m3") @ unpack_weight(phi_words, phi_scales, "e4m3")
    tr = vis * refl * f64(q)[None, :]
    rad = mxq(f64(l), 1, "e4m3") @ unpack_weight(theta_words, theta_scales, "e4m3")
    coef = 4.0 * np.pi / num_dirs
    return coef * (mxq(tr, 1, "e4m3") @ mxq(rad, 1, "e4m3").T)


def setup_inputs():
    drawn = draw0()
    full = np.asarray(drawn['v']).astype(np.float64)
    scale = (np.abs(full).reshape(8, 128, 4, 128).max(axis=(1, 3)) / 448.0).astype(np.float32)
    given = {}
    for key, value in drawn.items():
        if key == 'v':
            given['v_bytes'] = e4m3fn_bytes(full / np.repeat(np.repeat(scale.astype(np.float64), 128, axis=0), 128, axis=1))
            given['v_scale'] = scale
        else:
            given[key] = value
    return given


def reference(v_bytes, v_scale, psi_words, psi_scales, r, phi_words, phi_scales, q, l, theta_words, theta_scales):
    return core(e4m3fn_values(v_bytes) * np.repeat(np.repeat(v_scale.astype(np.float64), 128, axis=0), 128, axis=1), psi_words, psi_scales, r, phi_words, phi_scales, q, l, theta_words, theta_scales)

import math
from contextlib import ExitStack

import concourse.mybir as mybir
from concourse.masks import make_identity

F32 = mybir.dt.float32
BF16 = mybir.dt.bfloat16
I32 = mybir.dt.int32
U32 = mybir.dt.uint32
U8 = mybir.dt.uint8
E4M3 = mybir.dt.float8_e4m3fn
E4M3X4 = mybir.dt.float8_e4m3fn_x4
MULT = mybir.AluOpType.mult
ACT = mybir.ActivationFunctionType

P = 128
POINTS, K, DIRS, ENVS = 1024, 512, 1024, 512
HALF = 512
NT, NA, NR, NO = 2, 2, 2, 2
ORDER = [
    (("wid", 0, 0), "V"),
    (("wid", 0, 1), "V"),
    (("Tv", 0), "P"),
    (("Tv", 1), "P"),
    (("pw", "psi"), "V"),
    (("ev", 0), "S"),
    (("ev", 1), "V"),
    (("ev", 2), "S"),
    (("ev", 3), "V"),
    (("Tl", 0), "P"),
    (("Tl", 1), "P"),
    (("el", 0), "S"),
    (("el", 1), "S"),
    (("pp", "psi"), "V"),
    (("qv", 0), "V"),
    (("pw", "theta"), "V"),
    (("ql",), "V"),
    (("pp", "rest"), "V"),
    (("A", 0, 0), "P"),
    (("A", 0, 1), "P"),
    (("sig", 0, 0), "S"),
    (("A", 0, 2), "P"),
    (("sig", 0, 1), "S"),
    (("A", 0, 3), "P"),
    (("D", 0, 0), "P"),
    (("sig", 0, 2), "S"),
    (("A", 0, 4), "P"),
    (("D", 1, 0), "P"),
    (("sig", 0, 3), "S"),
    (("wt", 0, 0), "V"),
    (("re", 0, 0), "S"),
    (("wid", 1, 0), "V"),
    (("Tv", 2), "P"),
    (("wt", 0, 1), "V"),
    (("A", 0, 5), "P"),
    (("D", 2, 0), "P"),
    (("sig", 0, 4), "S"),
    (("re", 1, 0), "S"),
    (("wid", 1, 1), "V"),
    (("wt", 0, 2), "V"),
    (("ev", 4), "V"),
    (("pw", "phi"), "V"),
    (("D", 3, 0), "P"),
    (("A", 0, 6), "P"),
    (("sig", 0, 5), "S"),
    (("re", 2, 0), "V"),
    (("Tv", 3), "P"),
    (("wt", 0, 3), "S"),
    (("ev", 5), "V"),
    (("re", 3, 0), "V"),
    (("D", 0, 1), "P"),
    (("ev", 6), "V"),
    (("wt", 0, 4), "V"),
    (("sig", 0, 6), "S"),
    (("A", 0, 7), "P"),
    (("ev", 7), "V"),
    (("wt", 0, 5), "S"),
    (("re", 0, 1), "S"),
    (("D", 1, 1), "P"),
    (("sig", 0, 7), "S"),
    (("Tr", 0), "P"),
    (("Tr", 1), "P"),
    (("wt", 0, 6), "V"),
    (("re", 1, 1), "V"),
    (("D", 2, 1), "P"),
    (("er", 0), "S"),
    (("er", 1), "S"),
    (("wt", 0, 7), "V"),
    (("re", 2, 1), "S"),
    (("D", 3, 1), "P"),
    (("Tr", 2), "P"),
    (("qv", 1), "V"),
    (("re", 3, 1), "S"),
    (("qr", 0), "V"),
    (("rq", 0), "V"),
    (("A", 1, 0), "P"),
    (("R", 0, 0), "P"),
    (("rq", 1), "V"),
    (("sig", 1, 0), "S"),
    (("A", 1, 1), "P"),
    (("er", 2), "S"),
    (("R", 0, 1), "P"),
    (("tt", 0, 0), "V"),
    (("Tr", 3), "P"),
    (("sig", 1, 1), "S"),
    (("R", 1, 0), "P"),
    (("A", 1, 2), "P"),
    (("er", 3), "S"),
    (("tt", 0, 1), "V"),
    (("wt", 1, 0), "S"),
    (("sig", 1, 2), "S"),
    (("R", 1, 1), "P"),
    (("tt", 1, 0), "V"),
    (("A", 1, 3), "P"),
    (("wt", 1, 1), "S"),
    (("tt", 1, 1), "V"),
    (("R", 2, 0), "P"),
    (("sig", 1, 3), "S"),
    (("A", 1, 4), "P"),
    (("qr", 1), "V"),
    (("tt", 2, 0), "V"),
    (("wt", 1, 2), "S"),
    (("R", 2, 1), "P"),
    (("sig", 1, 4), "S"),
    (("tt", 2, 1), "V"),
    (("A", 1, 5), "P"),
    (("wt", 1, 3), "S"),
    (("R", 3, 0), "P"),
    (("tq", 0), "V"),
    (("tt", 3, 0), "V"),
    (("sig", 1, 5), "S"),
    (("wt", 1, 4), "V"),
    (("A", 1, 6), "P"),
    (("R", 3, 1), "P"),
    (("tt", 3, 1), "V"),
    (("R", 4, 0), "P"),
    (("tt", 4, 0), "V"),
    (("tq", 1), "V"),
    (("sig", 1, 6), "S"),
    (("wt", 1, 5), "V"),
    (("A", 1, 7), "P"),
    (("R", 4, 1), "P"),
    (("wt", 1, 6), "S"),
    (("sig", 1, 7), "S"),
    (("tq", 2), "V"),
    (("R", 5, 0), "P"),
    (("O", 0), "P"),
    (("tt", 5, 0), "V"),
    (("wt", 1, 7), "S"),
    (("tt", 4, 1), "V"),
    (("O", 1), "P"),
    (("tq", 3), "V"),
    (("oe", 0), "S"),
    (("R", 5, 1), "P"),
    (("tt", 5, 1), "V"),
    (("O", 2), "P"),
    (("oe", 1), "S"),
    (("R", 6, 0), "P"),
    (("O", 3), "P"),
    (("tt", 6, 0), "V"),
    (("oe", 2), "S"),
    (("R", 6, 1), "P"),
    (("tq", 4), "V"),
    (("tt", 6, 1), "V"),
    (("tq", 5), "V"),
    (("tq", 6), "V"),
    (("O", 4), "P"),
    (("oe", 3), "S"),
    (("R", 7, 0), "P"),
    (("tt", 7, 0), "V"),
    (("R", 7, 1), "P"),
    (("tt", 7, 1), "V"),
    (("O", 5), "P"),
    (("oe", 4), "S"),
    (("O", 6), "P"),
    (("tq7", 0), "V"),
    (("oe", 5), "S"),
    (("tq7", 1), "V"),
    (("oe", 6), "S"),
    (("O7", 0), "P"),
    (("O7", 1), "P"),
    (("oe7", 1), "V"),
    (("oe7", 0), "S"),
]
COEF = 4.0 * math.pi / DIRS
FLOPS = 2 * (2 * POINTS * K * DIRS + ENVS * K * DIRS + POINTS * DIRS * ENVS)


def tile_tripleproductvisibilityreflectancereligh_d2p_kernel(
    tc, v_bytes, v_scale, psi_words, psi_scales, r, phi_words, phi_scales, q, l, theta_words, theta_scales, out
):
    nc = tc.nc
    with ExitStack() as ctx:
        keep = ctx.enter_context(tc.tile_pool(name="keep", bufs=1))
        psum = ctx.enter_context(tc.psum_pool(name="psum", bufs=2))
        ctx.enter_context(tc.manual_schedule())

        def tile(shape, dtype, name):
            return keep.tile(shape, dtype, name=name, tag=name, align_bytes=256)

        def bank(kind, bufs):
            return psum.tile([P, 512], F32, name="bank_" + kind, tag=kind, bufs=bufs)

        warm = tile([P, 1], F32, "warm")
        ident = tile([P, P], F32, "ident")
        vsc_all = tile([P, 32], F32, "vsc_all")
        vsc = tile([P, 8], F32, "vsc")
        q_bf = tile([P, 2, 4], BF16, "q_bf")
        q_col = tile([P, 8], F32, "q_col")
        v_in = [tile([P, 4 * K], U8, "v_in%d" % h) for h in range(2)]
        v_wide = [tile([P, 4 * K], BF16, "v_wide%d" % h) for h in range(2)]
        r_in = [tile([P, 4 * K], BF16, "r_in%d" % h) for h in range(2)]
        l_in = tile([P, 4 * K], BF16, "l_in")
        raw_words = {n: tile([P, 2, 512], U32, "raw_" + n) for n in ("psi", "phi", "theta")}
        words = {n: tile([P, 2, 4, P], U32, "words_" + n) for n in ("psi", "phi", "theta")}
        raw_planes = {n: tile([P, DIRS], U8, "rawp_" + n) for n in ("psi", "rest")}
        planes = {n: tile([P, 2, 4, P], U8, "planes_" + n) for n in ("psi", "rest")}
        grouped = {n: tile([P, c * 512], BF16, "grouped_" + n) for n, c in (("v", 8), ("r", 8), ("l", 4))}
        codes = {n: tile([P, c * P], U32, "codes_" + n) for n, c in (("v", 8), ("r", 8), ("l", 4))}
        scl = {n: tile([P, c * P], U8, "scl_" + n) for n, c in (("v", 8), ("r", 8), ("l", 4))}
        vis = tile([P, 2, 4, POINTS], F32, "vis")
        tr = [tile([P, 2, P, 4], BF16, "tr%d" % m) for m in range(8)]
        tr_codes = [tile([P, 2, P], U32, "tr_codes%d" % m) for m in range(8)]
        tr_scl = [tile([P, 2, P], U8, "tr_scl%d" % m) for m in range(8)]
        rad = tile([P, 2, ENVS, 4], BF16, "rad")
        rad_codes = tile([P, 2, ENVS], U32, "rad_codes")
        rad_scl = tile([P, 2, ENVS], U8, "rad_scl")
        res = [tile([P, ENVS], F32, "res%d" % m) for m in range(8)]

        def load_words(name, src):
            nc.sync.dma_start(
                out=raw_words[name][:].rearrange("p g n -> p (g n)").bitcast(I32),
                in_=src.rearrange("o p n t -> p (o n t)").bitcast(I32),
            )

        PLANE = {"psi": ("psi", 0), "phi": ("rest", 0), "theta": ("rest", 4)}

        def load_planes(engine, name, src):
            rows = src.rearrange("o s n -> (o s) n")
            t, k = PLANE[name]
            for quad in range(4):
                engine.dma_start(
                    out=raw_planes[t][32 * quad + k : 32 * quad + k + 4, :].bitcast(I32),
                    in_=rows[4 * quad : 4 * quad + 4, :].bitcast(I32),
                )

        def load_half(dst, src, h):
            nc.sync.dma_start(
                out=dst[:].rearrange("p (i k) -> p i k", i=4),
                in_=src[HALF * h : HALF * (h + 1), :].rearrange("(i p) k -> p i k", p=P),
            )

        def permute_words(engine, name):
            engine.tensor_copy(
                out=words[name][:].bitcast(I32),
                in_=raw_words[name][:].bitcast(I32).rearrange("p g (m j) -> p g j m", j=4),
            )

        def permute_plane(engine, t):
            engine.tensor_copy(out=planes[t][:], in_=raw_planes[t][:].rearrange("p (g m j) -> p g j m", g=2, j=4))

        def widen(h, c, engine):
            dst = v_wide[h][:, 2 * K * c : 2 * K * (c + 1)]
            src = v_in[h][:, 2 * K * c : 2 * K * (c + 1)].bitcast(E4M3)
            if engine is nc.scalar:
                nc.scalar.copy(out=dst, in_=src)
            else:
                nc.vector.tensor_copy(out=dst, in_=src)

        def turn(tile_in, c):
            pt = bank("T", NT)
            w = tile_in[:, 2 * K * c : 2 * K * (c + 1)].bitcast(F32)
            for t in range(2):
                for u in range(2):
                    s = 2 * t + u
                    nc.tensor.transpose(pt[:, P * s : P * (s + 1)], w[:, 256 * t + u : 256 * (t + 1) : 2], ident[:])
            return pt

        def evac_v(engine, pt, k, t):
            i = 2 * k + t
            src = pt[:].bitcast(BF16).rearrange("p (t u r e) -> p t r u e", t=2, u=2, e=2)[:, t, :, :, :]
            dst = grouped["v"][:, 512 * i : 512 * (i + 1)].rearrange("p (r u e) -> p r u e", u=2, e=2)
            if engine is nc.scalar:
                nc.scalar.activation(out=dst, in_=src, func=ACT.Copy, scale=vsc[:, i : i + 1])
            else:
                nc.vector.tensor_scalar(out=dst, in0=src, scalar1=vsc[:, i : i + 1], scalar2=None, op0=MULT)

        def evac_words(engine, name, pt, k):
            src = pt[:].rearrange("p (t u r) -> p t r u", t=2, u=2)
            dst = grouped[name][:, 1024 * k : 1024 * (k + 1)].bitcast(F32).rearrange("p (t r u) -> p t r u", t=2, u=2)
            if engine is nc.scalar:
                nc.scalar.copy(out=dst, in_=src)
            else:
                nc.vector.tensor_copy(out=dst, in_=src)

        def quant(name, a, b):
            nc.vector.quantize_mx(
                out=codes[name][:, P * a : P * b].bitcast(E4M3X4),
                scales=scl[name][:, P * a : P * b],
                in_=grouped[name][:, 512 * a : 512 * b],
            )

        def mx(dst, weight, g, j, name, a, b):
            t, k = PLANE[weight]
            nc.tensor.matmul_mx(
                out=dst,
                lhsT=words[weight][:, g, j, :].bitcast(E4M3X4),
                lhsT_scale=planes[t][k:P, g, j, :],
                rhs=codes[name][:, P * a : P * b].bitcast(E4M3X4),
                rhs_scale=scl[name][:, P * a : P * b],
                start=True,
                stop=True,
            )

        def vis_mx(h, s):
            pa = bank("A", NA)
            mx(pa[:], "psi", s // 4, s % 4, "v", 4 * h, 4 * h + 4)
            return pa

        def sig(h, s, pa):
            nc.scalar.activation(out=vis[:, s // 4, s % 4, HALF * h : HALF * (h + 1)], in_=pa[:], func=ACT.Sigmoid)

        def weigh(engine, h, s):
            x = vis[:, s // 4, s % 4, HALF * h : HALF * (h + 1)]
            if engine is nc.scalar:
                nc.scalar.activation(out=x, in_=x, func=ACT.Copy, scale=q_col[:, s : s + 1])
            else:
                nc.vector.tensor_scalar(out=x, in0=x, scalar1=q_col[:, s : s + 1], scalar2=None, op0=MULT)

        def refl_mx(m, g):
            pr = bank("R", NR)
            for j in range(4):
                mx(pr[:, P * j : P * (j + 1)], "phi", g, j, "r", m, m + 1)
            return pr

        def tt(m, g, pr):
            nc.vector.tensor_tensor(
                out=tr[m][:, g, :, :],
                in0=pr[:].rearrange("p (j n) -> p n j", j=4),
                in1=vis[:, g, :, P * m : P * (m + 1)].rearrange("p j n -> p n j"),
                op=MULT,
            )

        def quant_tr(m, g=None):
            gs = slice(0, 2) if g is None else slice(g, g + 1)
            nc.vector.quantize_mx(
                out=tr_codes[m][:, gs, :].rearrange("p g n -> p (g n)").bitcast(E4M3X4),
                scales=tr_scl[m][:, gs, :].rearrange("p g n -> p (g n)"),
                in_=tr[m][:, gs, :, :].rearrange("p g n j -> p (g n j)"),
            )

        def rad_mx(i, g):
            pr = bank("R", NR)
            for j in range(4):
                mx(pr[:, P * j : P * (j + 1)], "theta", g, j, "l", i, i + 1)
            return pr

        def rad_evac(engine, i, g, pr):
            src = pr[:].rearrange("p (j n) -> p n j", j=4)
            dst = rad[:, g, P * i : P * (i + 1), :]
            if engine is nc.scalar:
                nc.scalar.copy(out=dst, in_=src)
            else:
                nc.vector.tensor_copy(out=dst, in_=src)

        def quant_rad(g):
            nc.vector.quantize_mx(
                out=rad_codes[:, g, :].bitcast(E4M3X4),
                scales=rad_scl[:, g, :],
                in_=rad[:, g, :, :].rearrange("p n j -> p (n j)"),
            )

        def out_mx(m, kind="O", a=0, b=ENVS):
            po = bank(kind, {"O": NO, "A": NA, "T": NT}[kind])
            for g in range(2):
                nc.tensor.matmul_mx(
                    out=po[:, 0 : b - a],
                    lhsT=tr_codes[m][:, g, :].bitcast(E4M3X4),
                    lhsT_scale=tr_scl[m][:, g, :],
                    rhs=rad_codes[:, g, a:b].bitcast(E4M3X4),
                    rhs_scale=rad_scl[:, g, a:b],
                    start=(g == 0),
                    stop=(g == 1),
                )
            return po

        def out_evac(engine, m, po, a, b):
            if engine is nc.scalar:
                nc.scalar.activation(out=res[m][:, a:b], in_=po[:, 0 : b - a], func=ACT.Copy, scale=COEF)
            else:
                nc.vector.tensor_scalar(out=res[m][:, a:b], in0=po[:, 0 : b - a], scalar1=COEF, scalar2=None, op0=MULT)
            nc.sync.dma_start(out=out[P * m : P * (m + 1), a:b], in_=res[m][:, a:b])

        S, V, G = nc.scalar, nc.vector, nc.gpsimd
        nc.gpsimd.dma_start(out=vsc_all[:], in_=v_scale.rearrange("i j -> (i j)").partition_broadcast(P))
        make_identity(nc, ident[:])
        nc.gpsimd.dma_start(out=q_bf[:], in_=q.rearrange("(g p j) -> p g j", g=2, j=4))
        for n in ("psi", "rest"):
            nc.vector.memset(raw_planes[n][:].bitcast(I32), 0)
        nc.vector.memset(warm[:], 0.0)

        for c in range(2):
            nc.sync.dma_start(
                out=v_in[0][:, 2 * K * c : 2 * K * (c + 1)].rearrange("p (i k) -> p i k", i=2),
                in_=v_bytes[256 * c : 256 * (c + 1), :].rearrange("(i p) k -> p i k", p=P),
            )
        load_planes(S, "psi", psi_scales)
        load_words("psi", psi_words)
        nc.scalar.activation(out=warm[:], in_=warm[:], func=ACT.Sigmoid)
        load_half(l_in, l, 0)
        load_planes(nc.sync, "theta", theta_scales)
        load_words("theta", theta_words)
        load_planes(nc.sync, "phi", phi_scales)
        load_half(v_in[1], v_bytes, 1)
        load_half(r_in[0], r, 0)
        load_words("phi", phi_words)
        load_half(r_in[1], r, 1)

        eng = {"V": V, "S": S, "G": G, "P": None}
        held = {}
        first = set()
        for step, on in ORDER:
            e = eng[on]
            what, args = step[0], step[1:]
            if what == "wid":
                widen(args[0], args[1], e)
            elif what == "Tv":
                held[step] = turn(v_wide[args[0] // 2], args[0] % 2)
            elif what == "Tr":
                held[step] = turn(r_in[args[0] // 2], args[0] % 2)
            elif what == "Tl":
                held[step] = turn(l_in, args[0])
            elif what == "ev":
                if "ev" not in first:
                    first.add("ev")
                    for jb in range(4):
                        nc.scalar.copy(
                            out=vsc[32 * jb : 32 * jb + 32, :],
                            in_=vsc_all[32 * jb : 32 * jb + 32, :].rearrange("p (i j) -> p j i", j=4)[:, jb, :],
                        )
                evac_v(e, held["Tv", args[0] // 2], args[0] // 2, args[0] % 2)
            elif what in ("er", "el"):
                evac_words(e, what[1], held["T" + what[1], args[0]], args[0])
            elif what in ("qv", "qr"):
                quant(what[1], 4 * args[0], 4 * args[0] + 4)
            elif what == "ql":
                quant("l", 0, 4)
            elif what == "pw":
                permute_words(e, args[0])
            elif what == "pp":
                permute_plane(e, args[0])
            elif what == "A":
                held[step] = vis_mx(args[0], args[1])
            elif what == "sig":
                sig(args[0], args[1], held["A", args[0], args[1]])
            elif what == "wt":
                if "wt" not in first:
                    first.add("wt")
                    nc.scalar.copy(out=q_col[:], in_=q_bf[:].rearrange("p g j -> p (g j)"))
                weigh(e, args[0], args[1])
            elif what == "R":
                held[step] = refl_mx(args[0], args[1])
            elif what == "tt":
                tt(args[0], args[1], held["R", args[0], args[1]])
            elif what == "tq":
                quant_tr(args[0])
            elif what == "tq7":
                quant_tr(7, args[0])
            elif what == "D":
                held[step] = rad_mx(args[0], args[1])
            elif what == "re":
                rad_evac(e, args[0], args[1], held["D", args[0], args[1]])
            elif what == "rq":
                quant_rad(args[0])
            elif what == "O":
                held[step] = out_mx(args[0])
            elif what == "O7":
                held[step] = out_mx(7, "O", 256 * args[0], 256 * args[0] + 256)
            elif what == "oe":
                out_evac(e, args[0], held["O", args[0]], 0, ENVS)
            elif what == "oe7":
                out_evac(e, 7, held["O7", args[0]], 256 * args[0], 256 * args[0] + 256)
